import numpy as np
import ml_dtypes


def mxq(x, axis, fmt="e4m3"):
    dtype, down = {"e4m3": (ml_dtypes.float8_e4m3fn, 7), "e5m2": (ml_dtypes.float8_e5m2, 14)}[fmt]
    v = np.moveaxis(np.asarray(x, np.float32).astype(ml_dtypes.bfloat16).astype(np.float64), axis, -1)
    blocks = v.reshape(v.shape[:-1] + (-1, 32))
    amax = np.abs(blocks).max(-1, keepdims=True)
    byte = np.maximum(np.where(amax > 0, np.frexp(amax)[1] - 1 + 127, 0) - down, 1)
    scale = np.exp2(byte - 127.0)
    codes = (blocks / scale).astype(np.float32).astype(dtype).astype(np.float64)
    return np.moveaxis((codes * scale).reshape(v.shape), -1, axis)


WIDE = False


def mx_kscale(k):
    if not WIDE:
        return np.ones(k)
    levels = np.array([30, -30])
    if k % 512:
        return np.exp2(np.random.permutation(np.resize(levels, k // 32))).repeat(32)
    a = np.empty((k // 512, 16))
    for p in range(k // 512):
        a[p, :8] = np.random.permutation(np.resize(levels, 8))
        for g in range(8):
            far = levels[np.abs(levels - a[p, g]) >= 10]
            a[p, g + 8] = far[np.random.randint(len(far))]
    return np.exp2(a.ravel()).repeat(32)


def f64(x):
    return np.asarray(x).astype(np.float64)


def striped(idx):
    return np.tile(np.asarray(idx).reshape(-1, 16).T, (8, 1)).astype(np.uint16)


def unstriped(offs):
    return offs[:16].T.reshape(-1).astype(np.int64)


def striped8(idx):
    return np.asarray(idx).reshape(8, -1, 16).transpose(0, 2, 1).reshape(128, -1).astype(np.uint16)


def unstriped8(offs):
    return offs.reshape(8, 16, -1).transpose(0, 2, 1).reshape(8, -1).astype(np.int64)


def pick8(x, idx, run):
    r = np.arange(len(x))
    return x[r[:, None], idx[r % (8 * run) // run]]


E2M1 = np.array([0.0, 0.5, 1.0, 1.5, 2.0, 3.0, 4.0, 6.0, -0.0, -0.5, -1.0, -1.5, -2.0, -3.0, -4.0, -6.0])


def pack_weight(w, fmt):
    k, n = w.shape
    w = f64(np.asarray(w, np.float32).astype(ml_dtypes.bfloat16)).reshape(k // 32, 32, n)
    amax = np.abs(w).max(1)
    if fmt in ("e4m3", "e5m2"):
        byte = np.frexp(amax)[1] - 1 + 127 - (7 if fmt == "e4m3" else 14)
    else:
        mant, ex = np.frexp(amax / 6.0)
        byte = np.where(mant > 0.5, ex, ex - 1) + 127
    byte = np.clip(np.where(amax > 0, byte, 1), 1, 254)
    scaled = (w * np.exp2(127.0 - byte)[:, None, :]).reshape(k, n).astype(np.float32)
    by_word = np.ascontiguousarray(scaled.reshape(k // 512, 128, 4, n).transpose(0, 1, 3, 2))
    if fmt in ("e4m3", "e5m2"):
        words = by_word.astype(ml_dtypes.float8_e4m3fn if fmt == "e4m3" else ml_dtypes.float8_e5m2).view(np.uint8)
    else:
        c = by_word.astype(ml_dtypes.float4_e2m1fn).view(np.uint8) & 0xF
        words = (c[..., 0::2] | (c[..., 1::2] << 4)).reshape(k // 512, 128, 2 * n)
    return np.ascontiguousarray(words), np.ascontiguousarray(byte.astype(np.uint8).reshape(k // 512, 16, n))


def unpack_weight(words, scales, fmt):
    g, _, n = scales.shape
    words = np.ascontiguousarray(words).reshape(g, 128, n, -1)
    if fmt in ("e4m3", "e5m2"):
        vals = words.view(ml_dtypes.float8_e4m3fn if fmt == "e4m3" else ml_dtypes.float8_e5m2).astype(np.float64)
    else:
        nib = np.empty((g, 128, n, 4), np.uint8)
        nib[..., 0::2] = words & 0xF
        nib[..., 1::2] = words >> 4
        vals = E2M1[nib]
    vals = vals * np.repeat(np.exp2(scales.astype(np.float64) - 127.0), 8, axis=1)[..., None]
    return vals.transpose(0, 1, 3, 2).reshape(g * 512, n)


K, T, J, R, C, S, U, E = 512, 1024, 256, 512, 512, 1024, 256, 512


def setup_inputs():
    n = np.random.standard_normal
    idx = np.random.permutation(T)[:J]
    idx2 = np.stack([np.random.permutation(C)[:J] for _ in range(8)])
    idx3 = np.random.permutation(S)[:U]
    idx4 = np.random.permutation(E)[:U]
    fk = mx_kscale(K)
    fr = mx_kscale(R)
    xtp = pack_weight(n((K, T)) / fk[:, None], "e5m2")
    wp = pack_weight(n((K, R)) * 1 / np.sqrt(K) * fk[:, None] * fr, "e2m1")
    vsp = pack_weight(n((R, S)) * 1 / np.sqrt(R) / fr[:, None], "e2m1")
    return {
        "xt_words": xtp[0],
        "xt_scales": xtp[1],
        "w_words": wp[0],
        "w_scales": wp[1],
        "vs_words": vsp[0],
        "vs_scales": vsp[1],
        "offs": striped(idx),
        "offs2": striped8(idx2),
        "offs3": striped(idx3),
        "offs4": striped(idx4),
    }


def reference(xt_words, xt_scales, w_words, w_scales, vs_words, vs_scales, offs, offs2, offs3, offs4):
    idx = unstriped(offs)
    idx2 = unstriped8(offs2)
    idx3 = unstriped(offs3)
    idx4 = unstriped(offs4)
    xtu = unpack_weight(xt_words, xt_scales, "e5m2")
    wu = unpack_weight(w_words, w_scales, "e2m1")
    vsu = unpack_weight(vs_words, vs_scales, "e2m1")
    xtidxg = xtu[:, idx]
    a = wu.T @ xtidxg
    pa = np.zeros((R, C))
    pa[np.arange(R)[:, None], idx2[np.arange(R) % 512 // 64]] = a
    paq = mxq(pa, 0, "e4m3")
    vsidx3g = vsu[:, idx3]
    p = paq.T @ vsidx3g
    y = np.zeros((C, E))
    y[:, idx4] = p
    return y

@@ -1,0 +1,167 @@
+from contextlib import ExitStack
+
+import concourse.mybir as mybir
+
+F32 = mybir.dt.float32
+BF16 = mybir.dt.bfloat16
+I32 = mybir.dt.int32
+U32 = mybir.dt.uint32
+U16 = mybir.dt.uint16
+U8 = mybir.dt.uint8
+E4M3 = mybir.dt.float8_e4m3fn_x4
+E5M2 = mybir.dt.float8_e5m2_x4
+E2M1 = mybir.dt.float4_e2m1fn_x4
+COPY = mybir.ActivationFunctionType.Copy
+
+P = 128
+PACK = 4
+QUADS = 4
+K, T, J, R, C, S, U, E = 512, 1024, 256, 512, 512, 1024, 256, 512
+FLOPS = 2 * K * R * J + 2 * R * C * U
+
+
+def tile_list_pagequeries_kernel(
+    tc, xt_words, xt_scales, w_words, w_scales, vs_words, vs_scales, offs, offs2, offs3, offs4, out
+):
+    nc = tc.nc
+    with ExitStack() as ctx:
+        lists = ctx.enter_context(tc.tile_pool(name="lists", bufs=1))
+        keep = ctx.enter_context(tc.tile_pool(name="keep", bufs=1))
+        psum = ctx.enter_context(tc.psum_pool(name="psum", bufs=1))
+
+        tok_list = lists.tile([P, J // 16], U16, name="tok_list")
+        board_list = lists.tile([P, J // 16], U16, name="board_list")
+        store_list = lists.tile([P, U // 16], U16, name="store_list")
+        page_list = lists.tile([P, U // 16], U16, name="page_list")
+
+        xt_w = keep.tile([P, T], U32, name="xt_w", align_bytes=64)
+        xt_s_rows = keep.tile([4, QUADS, T // 4], I32, name="xt_s_rows", align_bytes=64)
+        xt_s = keep.tile([P, T], U8, name="xt_s", align_bytes=64)
+        w_w = keep.tile([P, R], U16, name="w_w", align_bytes=64)
+        w_s_rows = keep.tile([4, QUADS, R // 4], I32, name="w_s_rows", align_bytes=64)
+        w_s = keep.tile([P, R], U8, name="w_s", align_bytes=64)
+        vs_w = keep.tile([P, S], U16, name="vs_w", align_bytes=64)
+        vs_s = keep.tile([P, S], U8, name="vs_s", align_bytes=64)
+
+        nc.scalar.dma_start(xt_s_rows[:], xt_scales[0].bitcast(I32).rearrange("(q r) n -> r q n", r=4))
+        nc.scalar.dma_start(w_s_rows[:], w_scales[0].bitcast(I32).rearrange("(q r) n -> r q n", r=4))
+        nc.sync.dma_start(tok_list[:], offs)
+        nc.sync.dma_start(xt_w[:].bitcast(I32), xt_words[0].rearrange("p n t -> p (n t)").bitcast(I32))
+        nc.sync.dma_start(w_w[:].bitcast(I32), w_words[0].bitcast(I32))
+        nc.sync.dma_start(board_list[:], offs2)
+        nc.sync.dma_start(store_list[:], offs3)
+        nc.sync.dma_start(page_list[:], offs4)
+
+        nc.vector.memset(xt_s[:].bitcast(I32), 0)
+        nc.vector.memset(w_s[:].bitcast(I32), 0)
+        nc.vector.memset(vs_s[:].bitcast(I32), 0)
+        boards = []
+        for t in range(2):
+            board = keep.tile([P, C], F32, name="board%d" % t, align_bytes=64)
+            nc.vector.memset(board[:], 0.0)
+            boards.append(board)
+
+        nc.sync.dma_start(vs_w[:].bitcast(I32), vs_words[0].bitcast(I32))
+        for q in range(QUADS):
+            nc.sync.dma_start(vs_s[32 * q : 32 * q + 4, :].bitcast(I32), vs_scales[0, 4 * q : 4 * q + 4, :].bitcast(I32))
+
+        for q in range(QUADS):
+            nc.vector.tensor_copy(xt_s[32 * q : 32 * q + 4, :].bitcast(I32), xt_s_rows[:, q, :])
+        for q in range(QUADS):
+            nc.vector.tensor_copy(w_s[32 * q : 32 * q + 4, :].bitcast(I32), w_s_rows[:, q, :])
+
+        xg_s = keep.tile([P, J], U8, name="xg_s", align_bytes=64)
+        nc.vector.tensor_copy(xg_s[:], xt_s[:].indirect(tok_list[:]))
+
+        w_w_by_t = w_w[:].rearrange("p (m t) -> p t m", t=PACK)
+        w_s_by_t = w_s[:].rearrange("p (m t) -> p t m", t=PACK)
+        xg_w = keep.tile([P, J], U32, name="xg_w", align_bytes=64)
+        grouped = keep.tile([P, C, PACK], BF16, name="grouped", align_bytes=64)
+
+        def deal(t):
+            lhs_s = keep.tile([P, P], U8, name="lhs_s%d" % t, align_bytes=64)
+            lhs_w = keep.tile([P, P], U16, name="lhs_w%d" % t, align_bytes=64)
+            nc.vector.tensor_copy(lhs_s[:], w_s_by_t[:, t, :])
+            nc.vector.tensor_copy(lhs_w[:], w_w_by_t[:, t, :])
+            return lhs_w, lhs_s
+
+        def multiply(t, lhs):
+            acc = psum.tile([P, J], F32, name="hid_acc%d" % t)
+            nc.tensor.matmul_mx(
+                out=acc[:], lhsT=lhs[0][:].bitcast(E2M1), lhsT_scale=lhs[1][:],
+                rhs=xg_w[:].bitcast(E5M2), rhs_scale=xg_s[:], start=True, stop=True,
+            )
+            return acc
+
+        def place(t, acc):
+            hid = keep.tile([P, J], F32, name="hid%d" % t, align_bytes=64)
+            nc.vector.tensor_copy(hid[:], acc[:])
+            nc.scalar.activation(boards[t % 2][:].indirect(board_list[:]), hid[:], COPY)
+
+        def widen(t):
+            nc.vector.tensor_copy(grouped[:, :, t], boards[t % 2][:])
+
+        vg_w = keep.tile([P, U], U16, name="vg_w", align_bytes=64)
+        vg_s = keep.tile([P, U], U8, name="vg_s", align_bytes=64)
+
+        lhs = deal(0)
+        nc.vector.tensor_copy(xg_w[:], xt_w[:].indirect(tok_list[:]))
+        place(0, multiply(0, lhs))
+        place(1, multiply(1, deal(1)))
+        acc2 = multiply(2, deal(2))
+        acc3 = multiply(3, deal(3))
+        nc.vector.tensor_copy(vg_w[:], vs_w[:].indirect(store_list[:]))
+        widen(0)
+        place(2, acc2)
+        nc.vector.tensor_copy(vg_s[:], vs_s[:].indirect(store_list[:]))
+        widen(1)
+        place(3, acc3)
+        widen(2)
+        pages = []
+        for b in range(C // P):
+            page = keep.tile([P, E], F32, name="page%d" % b, align_bytes=64)
+            nc.vector.memset(page[:], 0.0)
+            pages.append(page)
+
+        def cast(b):
+            cols = slice(b * P, (b + 1) * P)
+            nc.vector.tensor_copy(grouped[:, cols, PACK - 1], boards[1][:, cols])
+
+        def score(b):
+            cols = slice(b * P, (b + 1) * P)
+            codes = keep.tile([P, P], U32, name="codes%d" % b, align_bytes=64)
+            scales = keep.tile([P, P], U8, name="scales%d" % b, align_bytes=64)
+            nc.vector.quantize_mx(
+                out=codes[:].bitcast(E4M3), scales=scales[:],
+                in_=grouped[:, cols, :].rearrange("p c t -> p (c t)"),
+            )
+            acc = psum.tile([P, U], F32, name="score_acc%d" % b)
+            nc.tensor.matmul_mx(
+                out=acc[:], lhsT=codes[:].bitcast(E4M3), lhsT_scale=scales[:],
+                rhs=vg_w[:].bitcast(E2M1), rhs_scale=vg_s[:], start=True, stop=True,
+            )
+            return acc
+
+        accs = []
+        cast(0)
+        for b in range(C // P):
+            if b + 1 < C // P:
+                cast(b + 1)
+            accs.append(score(b))
+        scores = [keep.tile([P, U], F32, name="score%d" % b, align_bytes=64) for b in range(C // P)]
+
+        def store(b):
+            nc.sync.dma_start(out[b * P : (b + 1) * P, :], pages[b][:])
+
+        nc.scalar.copy(scores[0][:], accs[0][:])
+        nc.scalar.activation(pages[0][:].indirect(page_list[:]), scores[0][:], COPY)
+        store(0)
+        nc.vector.tensor_copy(scores[3][:], accs[3][:])
+        nc.vector.tensor_copy(pages[3][:].indirect(page_list[:]), scores[3][:])
+        store(3)
+        nc.scalar.copy(scores[1][:], accs[1][:])
+        nc.scalar.copy(scores[2][:], accs[2][:])
+        nc.scalar.activation(pages[1][:].indirect(page_list[:]), scores[1][:], COPY)
+        store(1)
+        nc.vector.tensor_copy(pages[2][:].indirect(page_list[:]), scores[2][:])
+        store(2)

@@ -16,6 +16,7 @@ COPY = mybir.ActivationFunctionType.Copy
 P = 128
 PACK = 4
 QUADS = 4
+PLANES = (2, 0, 1, 3)
 K, T, J, R, C, S, U, E = 512, 1024, 256, 512, 512, 1024, 256, 512
 FLOPS = 2 * K * R * J + 2 * R * C * U
 
@@ -34,7 +35,7 @@ def tile_list_pagequeries_kernel(
         store_list = lists.tile([P, U // 16], U16, name="store_list")
         page_list = lists.tile([P, U // 16], U16, name="page_list")
 
-        xt_w = keep.tile([P, T], U32, name="xt_w", align_bytes=64)
+        xt_w = keep.tile([P, T], U32, name="xt_w", tag="xt_w", align_bytes=64)
         xt_s_rows = keep.tile([4, QUADS, T // 4], I32, name="xt_s_rows", align_bytes=64)
         xt_s = keep.tile([P, T], U8, name="xt_s", align_bytes=64)
         w_w = keep.tile([P, R], U16, name="w_w", align_bytes=64)
@@ -58,96 +59,114 @@ def tile_list_pagequeries_kernel(
         boards = []
         for t in range(2):
             board = keep.tile([P, C], F32, name="board%d" % t, align_bytes=64)
-            nc.vector.memset(board[:], 0.0)
+            nc.vector.memset(board[:].bitcast(I32), 0)
             boards.append(board)
+        pages = {}
+        for b in (0, 1):
+            pages[b] = keep.tile([P, E], F32, name="page%d" % b, align_bytes=64)
+            nc.vector.memset(pages[b][:].bitcast(I32), 0)
 
         nc.sync.dma_start(vs_w[:].bitcast(I32), vs_words[0].bitcast(I32))
         for q in range(QUADS):
             nc.sync.dma_start(vs_s[32 * q : 32 * q + 4, :].bitcast(I32), vs_scales[0, 4 * q : 4 * q + 4, :].bitcast(I32))
 
         for q in range(QUADS):
-            nc.vector.tensor_copy(xt_s[32 * q : 32 * q + 4, :].bitcast(I32), xt_s_rows[:, q, :])
-        for q in range(QUADS):
             nc.vector.tensor_copy(w_s[32 * q : 32 * q + 4, :].bitcast(I32), w_s_rows[:, q, :])
+        for q in range(QUADS):
+            nc.vector.tensor_copy(xt_s[32 * q : 32 * q + 4, :].bitcast(I32), xt_s_rows[:, q, :])
 
         xg_s = keep.tile([P, J], U8, name="xg_s", align_bytes=64)
-        nc.vector.tensor_copy(xg_s[:], xt_s[:].indirect(tok_list[:]))
 
         w_w_by_t = w_w[:].rearrange("p (m t) -> p t m", t=PACK)
         w_s_by_t = w_s[:].rearrange("p (m t) -> p t m", t=PACK)
         xg_w = keep.tile([P, J], U32, name="xg_w", align_bytes=64)
-        grouped = keep.tile([P, C, PACK], BF16, name="grouped", align_bytes=64)
+        grouped = [keep.tile([P, P, PACK], BF16, name="grouped%d" % b, align_bytes=64) for b in range(C // P)]
 
         def deal(t):
             lhs_s = keep.tile([P, P], U8, name="lhs_s%d" % t, align_bytes=64)
             lhs_w = keep.tile([P, P], U16, name="lhs_w%d" % t, align_bytes=64)
-            nc.vector.tensor_copy(lhs_s[:], w_s_by_t[:, t, :])
-            nc.vector.tensor_copy(lhs_w[:], w_w_by_t[:, t, :])
+            nc.vector.tensor_copy(lhs_s[:], w_s_by_t[:, PLANES[t], :])
+            nc.vector.tensor_copy(lhs_w[:], w_w_by_t[:, PLANES[t], :])
             return lhs_w, lhs_s
 
         def multiply(t, lhs):
-            acc = psum.tile([P, J], F32, name="hid_acc%d" % t)
+            acc = psum.tile([P, J], F32, name="hid_acc%d" % t, tag="bank%d" % (t + 1))
             nc.tensor.matmul_mx(
                 out=acc[:], lhsT=lhs[0][:].bitcast(E2M1), lhsT_scale=lhs[1][:],
                 rhs=xg_w[:].bitcast(E5M2), rhs_scale=xg_s[:], start=True, stop=True,
             )
             return acc
 
-        def place(t, acc):
-            hid = keep.tile([P, J], F32, name="hid%d" % t, align_bytes=64)
+        def fetch(t, acc):
+            hid = keep.tile([P, J], F32, name="hid%d" % t, tag="hid%d" % t, align_bytes=64)
             nc.vector.tensor_copy(hid[:], acc[:])
+            return hid
+
+        def place(t, hid):
             nc.scalar.activation(boards[t % 2][:].indirect(board_list[:]), hid[:], COPY)
 
-        def widen(t):
-            nc.vector.tensor_copy(grouped[:, :, t], boards[t % 2][:])
+        def clear_page(b, tag):
+            pages[b] = keep.tile([P, E], F32, name="page%d" % b, tag=tag, align_bytes=64)
+            nc.vector.memset(pages[b][:].bitcast(I32), 0)
+
+        def widen(n):
+            for b in range(C // P):
+                nc.vector.tensor_copy(grouped[b][:, :, PLANES[n]], boards[n % 2][:, b * P : (b + 1) * P])
 
         vg_w = keep.tile([P, U], U16, name="vg_w", align_bytes=64)
         vg_s = keep.tile([P, U], U8, name="vg_s", align_bytes=64)
 
         lhs = deal(0)
-        nc.vector.tensor_copy(xg_w[:], xt_w[:].indirect(tok_list[:]))
-        place(0, multiply(0, lhs))
-        place(1, multiply(1, deal(1)))
-        acc2 = multiply(2, deal(2))
-        acc3 = multiply(3, deal(3))
+        for h in range(2):
+            slots = slice(h * P, (h + 1) * P)
+            entries = slice(h * P // 16, (h + 1) * P // 16)
+            nc.vector.tensor_copy(xg_s[:, slots], xt_s[:].indirect(tok_list[:, entries]))
+            nc.vector.tensor_copy(xg_w[:, slots], xt_w[:].indirect(tok_list[:, entries]))
+            half_acc = psum.tile([P, P], F32, name="half_acc%d" % h, tag="bank%d" % h)
+            nc.tensor.matmul_mx(
+                out=half_acc[:], lhsT=lhs[0][:].bitcast(E2M1), lhsT_scale=lhs[1][:],
+                rhs=xg_w[:, slots].bitcast(E5M2), rhs_scale=xg_s[:, slots], start=True, stop=True,
+            )
+            half = keep.tile([P, P], F32, name="half%d" % h, align_bytes=64)
+            nc.vector.tensor_copy(half[:], half_acc[:])
+            nc.scalar.activation(boards[0][:].indirect(board_list[:, entries]), half[:], COPY)
+        place(1, fetch(1, multiply(1, deal(1))))
+        hid2 = fetch(2, multiply(2, deal(2)))
+        hid3 = fetch(3, multiply(3, deal(3)))
         nc.vector.tensor_copy(vg_w[:], vs_w[:].indirect(store_list[:]))
         widen(0)
-        place(2, acc2)
+        place(2, hid2)
         nc.vector.tensor_copy(vg_s[:], vs_s[:].indirect(store_list[:]))
         widen(1)
-        place(3, acc3)
+        place(3, hid3)
+        clear_page(2, "xt_w")
+        clear_page(3, "hid1")
         widen(2)
-        pages = []
-        for b in range(C // P):
-            page = keep.tile([P, E], F32, name="page%d" % b, align_bytes=64)
-            nc.vector.memset(page[:], 0.0)
-            pages.append(page)
 
         def cast(b):
             cols = slice(b * P, (b + 1) * P)
-            nc.vector.tensor_copy(grouped[:, cols, PACK - 1], boards[1][:, cols])
+            if b < 2:
+                nc.vector.tensor_copy(grouped[b][:, :, PACK - 1], boards[1][:, cols])
+            else:
+                nc.scalar.copy(grouped[b][:, :, PACK - 1], boards[1][:, cols])
 
         def score(b):
-            cols = slice(b * P, (b + 1) * P)
             codes = keep.tile([P, P], U32, name="codes%d" % b, align_bytes=64)
             scales = keep.tile([P, P], U8, name="scales%d" % b, align_bytes=64)
             nc.vector.quantize_mx(
                 out=codes[:].bitcast(E4M3), scales=scales[:],
-                in_=grouped[:, cols, :].rearrange("p c t -> p (c t)"),
+                in_=grouped[b][:].rearrange("p c t -> p (c t)"),
             )
-            acc = psum.tile([P, U], F32, name="score_acc%d" % b)
+            acc = psum.tile([P, U], F32, name="score_acc%d" % b, tag="bank%d" % ((b + 5) % 8))
             nc.tensor.matmul_mx(
                 out=acc[:], lhsT=codes[:].bitcast(E4M3), lhsT_scale=scales[:],
                 rhs=vg_w[:].bitcast(E2M1), rhs_scale=vg_s[:], start=True, stop=True,
             )
             return acc
 
-        accs = []
-        cast(0)
         for b in range(C // P):
-            if b + 1 < C // P:
-                cast(b + 1)
-            accs.append(score(b))
+            cast(b)
+        accs = [score(b) for b in range(C // P)]
         scores = [keep.tile([P, U], F32, name="score%d" % b, align_bytes=64) for b in range(C // P)]
 
         def store(b):
@@ -156,12 +175,12 @@ def tile_list_pagequeries_kernel(
         nc.scalar.copy(scores[0][:], accs[0][:])
         nc.scalar.activation(pages[0][:].indirect(page_list[:]), scores[0][:], COPY)
         store(0)
-        nc.vector.tensor_copy(scores[3][:], accs[3][:])
-        nc.vector.tensor_copy(pages[3][:].indirect(page_list[:]), scores[3][:])
-        store(3)
-        nc.scalar.copy(scores[1][:], accs[1][:])
-        nc.scalar.copy(scores[2][:], accs[2][:])
-        nc.scalar.activation(pages[1][:].indirect(page_list[:]), scores[1][:], COPY)
+        nc.vector.tensor_copy(scores[1][:], accs[1][:])
+        nc.vector.tensor_copy(pages[1][:].indirect(page_list[:]), scores[1][:])
         store(1)
+        nc.vector.tensor_copy(scores[2][:], accs[2][:])
         nc.vector.tensor_copy(pages[2][:].indirect(page_list[:]), scores[2][:])
+        nc.scalar.copy(scores[3][:], accs[3][:])
+        nc.scalar.activation(pages[3][:].indirect(page_list[:]), scores[3][:], COPY)
         store(2)
+        nc.scalar.dma_start(out[3 * P : 4 * P, :], pages[3][:])

from contextlib import ExitStack

import concourse.mybir as mybir

F32 = mybir.dt.float32
BF16 = mybir.dt.bfloat16
I32 = mybir.dt.int32
U32 = mybir.dt.uint32
U16 = mybir.dt.uint16
U8 = mybir.dt.uint8
E4M3 = mybir.dt.float8_e4m3fn_x4
E5M2 = mybir.dt.float8_e5m2_x4
E2M1 = mybir.dt.float4_e2m1fn_x4
COPY = mybir.ActivationFunctionType.Copy

P = 128
PACK = 4
QUADS = 4
PLANES = (2, 0, 1, 3)
K, T, J, R, C, S, U, E = 512, 1024, 256, 512, 512, 1024, 256, 512
FLOPS = 2 * K * R * J + 2 * R * C * U


def tile_list_pagequeries_kernel(
    tc, xt_words, xt_scales, w_words, w_scales, vs_words, vs_scales, offs, offs2, offs3, offs4, out
):
    nc = tc.nc
    with ExitStack() as ctx:
        lists = ctx.enter_context(tc.tile_pool(name="lists", bufs=1))
        keep = ctx.enter_context(tc.tile_pool(name="keep", bufs=1))
        psum = ctx.enter_context(tc.psum_pool(name="psum", bufs=1))

        tok_list = lists.tile([P, J // 16], U16, name="tok_list")
        board_list = lists.tile([P, J // 16], U16, name="board_list")
        store_list = lists.tile([P, U // 16], U16, name="store_list")
        page_list = lists.tile([P, U // 16], U16, name="page_list")

        xt_w = keep.tile([P, T], U32, name="xt_w", tag="xt_w", align_bytes=64)
        xt_s_rows = keep.tile([4, QUADS, T // 4], I32, name="xt_s_rows", align_bytes=64)
        xt_s = keep.tile([P, T], U8, name="xt_s", align_bytes=64)
        w_w = keep.tile([P, R], U16, name="w_w", align_bytes=64)
        w_s_rows = keep.tile([4, QUADS, R // 4], I32, name="w_s_rows", align_bytes=64)
        w_s = keep.tile([P, R], U8, name="w_s", align_bytes=64)
        vs_w = keep.tile([P, S], U16, name="vs_w", align_bytes=64)
        vs_s = keep.tile([P, S], U8, name="vs_s", align_bytes=64)

        nc.scalar.dma_start(xt_s_rows[:], xt_scales[0].bitcast(I32).rearrange("(q r) n -> r q n", r=4))
        nc.scalar.dma_start(w_s_rows[:], w_scales[0].bitcast(I32).rearrange("(q r) n -> r q n", r=4))
        nc.sync.dma_start(tok_list[:], offs)
        nc.sync.dma_start(xt_w[:].bitcast(I32), xt_words[0].rearrange("p n t -> p (n t)").bitcast(I32))
        nc.sync.dma_start(w_w[:].bitcast(I32), w_words[0].bitcast(I32))
        nc.sync.dma_start(board_list[:], offs2)
        nc.sync.dma_start(store_list[:], offs3)
        nc.sync.dma_start(page_list[:], offs4)

        nc.vector.memset(xt_s[:].bitcast(I32), 0)
        nc.vector.memset(w_s[:].bitcast(I32), 0)
        nc.vector.memset(vs_s[:].bitcast(I32), 0)
        boards = []
        for t in range(2):
            board = keep.tile([P, C], F32, name="board%d" % t, align_bytes=64)
            nc.vector.memset(board[:].bitcast(I32), 0)
            boards.append(board)
        pages = {}
        for b in (0, 1):
            pages[b] = keep.tile([P, E], F32, name="page%d" % b, align_bytes=64)
            nc.vector.memset(pages[b][:].bitcast(I32), 0)

        nc.sync.dma_start(vs_w[:].bitcast(I32), vs_words[0].bitcast(I32))
        for q in range(QUADS):
            nc.sync.dma_start(vs_s[32 * q : 32 * q + 4, :].bitcast(I32), vs_scales[0, 4 * q : 4 * q + 4, :].bitcast(I32))

        for q in range(QUADS):
            nc.vector.tensor_copy(w_s[32 * q : 32 * q + 4, :].bitcast(I32), w_s_rows[:, q, :])
        for q in range(QUADS):
            nc.vector.tensor_copy(xt_s[32 * q : 32 * q + 4, :].bitcast(I32), xt_s_rows[:, q, :])

        xg_s = keep.tile([P, J], U8, name="xg_s", align_bytes=64)

        w_w_by_t = w_w[:].rearrange("p (m t) -> p t m", t=PACK)
        w_s_by_t = w_s[:].rearrange("p (m t) -> p t m", t=PACK)
        xg_w = keep.tile([P, J], U32, name="xg_w", align_bytes=64)
        grouped = [keep.tile([P, P, PACK], BF16, name="grouped%d" % b, align_bytes=64) for b in range(C // P)]

        def deal(t):
            lhs_s = keep.tile([P, P], U8, name="lhs_s%d" % t, align_bytes=64)
            lhs_w = keep.tile([P, P], U16, name="lhs_w%d" % t, align_bytes=64)
            nc.vector.tensor_copy(lhs_s[:], w_s_by_t[:, PLANES[t], :])
            nc.vector.tensor_copy(lhs_w[:], w_w_by_t[:, PLANES[t], :])
            return lhs_w, lhs_s

        def multiply(t, lhs):
            acc = psum.tile([P, J], F32, name="hid_acc%d" % t, tag="bank%d" % (t + 1))
            nc.tensor.matmul_mx(
                out=acc[:], lhsT=lhs[0][:].bitcast(E2M1), lhsT_scale=lhs[1][:],
                rhs=xg_w[:].bitcast(E5M2), rhs_scale=xg_s[:], start=True, stop=True,
            )
            return acc

        def fetch(t, acc):
            hid = keep.tile([P, J], F32, name="hid%d" % t, tag="hid%d" % t, align_bytes=64)
            nc.vector.tensor_copy(hid[:], acc[:])
            return hid

        def place(t, hid):
            nc.scalar.activation(boards[t % 2][:].indirect(board_list[:]), hid[:], COPY)

        def clear_page(b, tag):
            pages[b] = keep.tile([P, E], F32, name="page%d" % b, tag=tag, align_bytes=64)
            nc.vector.memset(pages[b][:].bitcast(I32), 0)

        def widen(n):
            for b in range(C // P):
                nc.vector.tensor_copy(grouped[b][:, :, PLANES[n]], boards[n % 2][:, b * P : (b + 1) * P])

        vg_w = keep.tile([P, U], U16, name="vg_w", align_bytes=64)
        vg_s = keep.tile([P, U], U8, name="vg_s", align_bytes=64)

        lhs = deal(0)
        for h in range(2):
            slots = slice(h * P, (h + 1) * P)
            entries = slice(h * P // 16, (h + 1) * P // 16)
            nc.vector.tensor_copy(xg_s[:, slots], xt_s[:].indirect(tok_list[:, entries]))
            nc.vector.tensor_copy(xg_w[:, slots], xt_w[:].indirect(tok_list[:, entries]))
            half_acc = psum.tile([P, P], F32, name="half_acc%d" % h, tag="bank%d" % h)
            nc.tensor.matmul_mx(
                out=half_acc[:], lhsT=lhs[0][:].bitcast(E2M1), lhsT_scale=lhs[1][:],
                rhs=xg_w[:, slots].bitcast(E5M2), rhs_scale=xg_s[:, slots], start=True, stop=True,
            )
            half = keep.tile([P, P], F32, name="half%d" % h, align_bytes=64)
            nc.vector.tensor_copy(half[:], half_acc[:])
            nc.scalar.activation(boards[0][:].indirect(board_list[:, entries]), half[:], COPY)
        place(1, fetch(1, multiply(1, deal(1))))
        hid2 = fetch(2, multiply(2, deal(2)))
        hid3 = fetch(3, multiply(3, deal(3)))
        nc.vector.tensor_copy(vg_w[:], vs_w[:].indirect(store_list[:]))
        widen(0)
        place(2, hid2)
        nc.vector.tensor_copy(vg_s[:], vs_s[:].indirect(store_list[:]))
        widen(1)
        place(3, hid3)
        clear_page(2, "xt_w")
        clear_page(3, "hid1")
        widen(2)

        def cast(b):
            cols = slice(b * P, (b + 1) * P)
            if b < 2:
                nc.vector.tensor_copy(grouped[b][:, :, PACK - 1], boards[1][:, cols])
            else:
                nc.scalar.copy(grouped[b][:, :, PACK - 1], boards[1][:, cols])

        def score(b):
            codes = keep.tile([P, P], U32, name="codes%d" % b, align_bytes=64)
            scales = keep.tile([P, P], U8, name="scales%d" % b, align_bytes=64)
            nc.vector.quantize_mx(
                out=codes[:].bitcast(E4M3), scales=scales[:],
                in_=grouped[b][:].rearrange("p c t -> p (c t)"),
            )
            acc = psum.tile([P, U], F32, name="score_acc%d" % b, tag="bank%d" % ((b + 5) % 8))
            nc.tensor.matmul_mx(
                out=acc[:], lhsT=codes[:].bitcast(E4M3), lhsT_scale=scales[:],
                rhs=vg_w[:].bitcast(E2M1), rhs_scale=vg_s[:], start=True, stop=True,
            )
            return acc

        for b in range(C // P):
            cast(b)
        accs = [score(b) for b in range(C // P)]
        scores = [keep.tile([P, U], F32, name="score%d" % b, align_bytes=64) for b in range(C // P)]

        def store(b):
            nc.sync.dma_start(out[b * P : (b + 1) * P, :], pages[b][:])

        nc.scalar.copy(scores[0][:], accs[0][:])
        nc.scalar.activation(pages[0][:].indirect(page_list[:]), scores[0][:], COPY)
        store(0)
        nc.vector.tensor_copy(scores[1][:], accs[1][:])
        nc.vector.tensor_copy(pages[1][:].indirect(page_list[:]), scores[1][:])
        store(1)
        nc.vector.tensor_copy(scores[2][:], accs[2][:])
        nc.vector.tensor_copy(pages[2][:].indirect(page_list[:]), scores[2][:])
        nc.scalar.copy(scores[3][:], accs[3][:])
        nc.scalar.activation(pages[3][:].indirect(page_list[:]), scores[3][:], COPY)
        store(2)
        nc.scalar.dma_start(out[3 * P : 4 * P, :], pages[3][:])
